import numpy as np
import ml_dtypes


def mxq(x, axis, fmt="e4m3"):
    dtype, down = {"e4m3": (ml_dtypes.float8_e4m3fn, 7), "e5m2": (ml_dtypes.float8_e5m2, 14)}[fmt]
    v = np.moveaxis(np.asarray(x, np.float32).astype(ml_dtypes.bfloat16).astype(np.float64), axis, -1)
    blocks = v.reshape(v.shape[:-1] + (-1, 32))
    amax = np.abs(blocks).max(-1, keepdims=True)
    byte = np.maximum(np.where(amax > 0, np.frexp(amax)[1] - 1 + 127, 0) - down, 1)
    scale = np.exp2(byte - 127.0)
    codes = (blocks / scale).astype(np.float32).astype(dtype).astype(np.float64)
    return np.moveaxis((codes * scale).reshape(v.shape), -1, axis)


WIDE = False


def mx_kscale(k):
    if not WIDE:
        return np.ones(k)
    levels = np.array([10, -10, 5, -5, 0])
    if k % 512:
        return np.exp2(np.random.permutation(np.resize(levels, k // 32))).repeat(32)
    a = np.empty((k // 512, 16))
    for p in range(k // 512):
        a[p, :8] = np.random.permutation(np.resize(levels, 8))
        for g in range(8):
            far = levels[np.abs(levels - a[p, g]) >= 10]
            a[p, g + 8] = far[np.random.randint(len(far))]
    return np.exp2(a.ravel()).repeat(32)


def f64(x):
    return np.asarray(x).astype(np.float64)


def striped(idx):
    return np.tile(np.asarray(idx).reshape(-1, 16).T, (8, 1)).astype(np.uint16)


def unstriped(offs):
    return offs[:16].T.reshape(-1).astype(np.int64)


E2M1 = np.array([0.0, 0.5, 1.0, 1.5, 2.0, 3.0, 4.0, 6.0, -0.0, -0.5, -1.0, -1.5, -2.0, -3.0, -4.0, -6.0])


def pack_weight(w, fmt):
    k, n = w.shape
    w = f64(np.asarray(w, np.float32).astype(ml_dtypes.bfloat16)).reshape(k // 32, 32, n)
    amax = np.abs(w).max(1)
    if fmt == "e4m3":
        byte = np.frexp(amax)[1] - 1 + 127 - 7
    else:
        mant, ex = np.frexp(amax / 6.0)
        byte = np.where(mant > 0.5, ex, ex - 1) + 127
    byte = np.clip(np.where(amax > 0, byte, 1), 1, 254)
    scaled = (w * np.exp2(127.0 - byte)[:, None, :]).reshape(k, n).astype(np.float32)
    by_word = np.ascontiguousarray(scaled.reshape(k // 512, 128, 4, n).transpose(0, 1, 3, 2))
    if fmt == "e4m3":
        words = by_word.astype(ml_dtypes.float8_e4m3fn).view(np.uint8)
    else:
        c = by_word.astype(ml_dtypes.float4_e2m1fn).view(np.uint8) & 0xF
        words = (c[..., 0::2] | (c[..., 1::2] << 4)).reshape(k // 512, 128, 2 * n)
    return np.ascontiguousarray(words), np.ascontiguousarray(byte.astype(np.uint8).reshape(k // 512, 16, n))


def unpack_weight(words, scales, fmt):
    g, _, n = scales.shape
    words = np.ascontiguousarray(words).reshape(g, 128, n, -1)
    if fmt == "e4m3":
        vals = words.view(ml_dtypes.float8_e4m3fn).astype(np.float64)
    else:
        nib = np.empty((g, 128, n, 4), np.uint8)
        nib[..., 0::2] = words & 0xF
        nib[..., 1::2] = words >> 4
        vals = E2M1[nib]
    vals = vals * np.repeat(np.exp2(scales.astype(np.float64) - 127.0), 8, axis=1)[..., None]
    return vals.transpose(0, 1, 3, 2).reshape(g * 512, n)


def sigmoid(v):
    return 1.0 / (1.0 + np.exp(-v))


K, R, F, T, J, G = 512, 128, 512, 2048, 512, 32


def setup_inputs():
    n = np.random.standard_normal
    idx = np.random.permutation(T)[:J]
    fk = mx_kscale(K)
    ff = mx_kscale(F)
    tabp = pack_weight(n((K, T)) / fk[:, None], "e4m3")
    return {
        "tab_words": tabp[0],
        "tab_scales": tabp[1],
        "w1": (n((K, R)) * 1 / np.sqrt(K) * fk[:, None]).astype(np.float32),
        "steep": (np.random.uniform(1.0, 4.0, (R, 1))).astype(np.float32),
        "bias": (np.random.uniform(-0.5, 0.5, (R, 1))).astype(np.float32),
        "wo": (n((F, R)) * 1 / np.sqrt(F) * ff[:, None]).astype(np.float32),
        "dy": (n((F, J)) / ff[:, None]).astype(np.float32),
        "old": (0.5 * n((R, J))).astype(np.float32),
        "offs": striped(idx),
    }


def reference(tab_words, tab_scales, w1, steep, bias, wo, dy, old, offs):
    idx = unstriped(offs)
    tabu = unpack_weight(tab_words, tab_scales, "e4m3")
    w1q = mxq(f64(w1), 0, "e4m3")
    tabidxg = tabu[:, idx]
    a = w1q.T @ tabidxg
    m1 = a.reshape(R, G, J // G).mean(axis=2)
    gt = sigmoid(m1 * f64(steep) + f64(bias))
    gr0 = np.repeat(gt, J // G, axis=1)
    woq = mxq(f64(wo), 0, "e4m3")
    dyq = mxq(f64(dy), 0, "e4m3")
    c0 = woq.T @ dyq
    dgr0 = c0 * a
    dgt = dgr0.reshape(R, G, J // G).sum(axis=2)
    dm1 = dgt * gt * (1.0 - gt) * f64(steep)
    e1 = dm1 / 16.0
    r1 = np.repeat(e1, J // G, axis=1)
    da = c0 * gr0 + r1
    y = da + f64(old)
    return y

@@ -1,0 +1,187 @@
+from contextlib import ExitStack
+
+import concourse.mybir as mybir
+
+K, R, F, T, J, G = 512, 128, 512, 2048, 512, 32
+FLOPS = 2 * K * R * J + 2 * F * R * J
+
+F32 = mybir.dt.float32
+BF16 = mybir.dt.bfloat16
+I32 = mybir.dt.int32
+U32 = mybir.dt.uint32
+U16 = mybir.dt.uint16
+U8 = mybir.dt.uint8
+FP8X4 = mybir.dt.float8_e4m3fn_x4
+ALU = mybir.AluOpType
+ACT = mybir.ActivationFunctionType
+AXIS_X = mybir.AxisListType.X
+
+P = 128
+PACK = 4
+GROUP = J // G
+HALF = J // 2
+QUARTER = J // 4
+
+
+def interleave(copy, grouped, raw):
+    copy(
+        out=grouped.rearrange("p (c i) t -> p c t i", i=4),
+        in_=raw.rearrange("p t (c i) -> p c t i", i=4),
+    )
+
+
+def quantize(nc, codes, scales, grouped):
+    nc.vector.quantize_mx(
+        out=codes.bitcast(FP8X4), scales=scales, in_=grouped.rearrange("p w t -> p (w t)")
+    )
+
+
+def by_group(ap):
+    return ap.rearrange("p (g i) -> p g i", i=GROUP)
+
+
+def spread(ap):
+    return ap.unsqueeze(2).to_broadcast([P, ap.shape[1], GROUP])
+
+
+def tile_attend_csqueeze_kernel(tc, tab_words, tab_scales, w1, steep, bias, wo, dy, old, offs, out):
+    nc = tc.nc
+    with ExitStack() as ctx:
+        keep = ctx.enter_context(tc.tile_pool(name="keep", bufs=1))
+        psum = ctx.enter_context(tc.psum_pool(name="psum", bufs=1))
+
+        offsets = keep.tile([P, J // 16], U16, name="offsets")
+        tab_s = keep.tile([P, T], U8, name="tab_s", align_bytes=64)
+        tab_w = keep.tile([P, T], U32, name="tab_w", align_bytes=64)
+        w1_raw = keep.tile([P, PACK, R], F32, name="w1_raw")
+        wo_raw = keep.tile([P, PACK, R], F32, name="wo_raw")
+        dy_raw = [keep.tile([P, PACK, HALF], F32, name="dy_raw%d" % h) for h in range(2)]
+        old_sb = keep.tile([P, J], F32, name="old_sb")
+        steep_sb = keep.tile([P, 1], F32, name="steep_sb")
+        bias_sb = keep.tile([P, 1], F32, name="bias_sb")
+        warm = keep.tile([P, 1], F32, name="warm")
+        warm_out = keep.tile([P, 1], F32, name="warm_out")
+
+        nc.vector.memset(tab_s[:].bitcast(I32), 0)
+        nc.sync.dma_start(offsets[:], offs)
+        scale_rows = tab_scales[0].bitcast(I32)
+        for q in (0, 2, 1, 3):
+            nc.scalar.dma_start(
+                tab_s[32 * q : 32 * q + 4, :].bitcast(I32), scale_rows[4 * q : 4 * q + 4, :]
+            )
+        nc.vector.memset(warm[:], 0.0)
+        nc.scalar.activation(warm_out[:], warm[:], ACT.Sigmoid)
+        nc.sync.dma_start(w1_raw[:], w1.rearrange("(p t) r -> p t r", t=PACK))
+        nc.sync.dma_start(
+            tab_w[:].bitcast(I32), tab_words[0].rearrange("p n t -> p (n t)").bitcast(I32)
+        )
+        nc.gpsimd.dma_start(steep_sb[:], steep)
+        nc.gpsimd.dma_start(bias_sb[:], bias)
+        nc.sync.dma_start(wo_raw[:], wo.rearrange("(p t) r -> p t r", t=PACK))
+        dy_planes = dy.rearrange("(p t) j -> p t j", t=PACK)
+        for h in range(2):
+            nc.sync.dma_start(dy_raw[h][:], dy_planes[:, :, h * HALF : (h + 1) * HALF])
+        nc.sync.dma_start(old_sb[:], old)
+
+        got_s = keep.tile([P, J], U8, name="got_s", align_bytes=64)
+        nc.vector.tensor_copy(got_s[:], tab_s[:].indirect(offsets[:]))
+
+        w1_bf = keep.tile([P, R, PACK], BF16, name="w1_bf", align_bytes=64)
+        w1_c = keep.tile([P, R], U32, name="w1_c", align_bytes=64)
+        w1_s = keep.tile([P, R], U8, name="w1_s", align_bytes=64)
+        interleave(nc.scalar.copy, w1_bf[:], w1_raw[:])
+        quantize(nc, w1_c[:], w1_s[:], w1_bf[:])
+
+        slope = keep.tile([P, 1], F32, name="slope")
+        neg_slope = keep.tile([P, 1], F32, name="neg_slope")
+        nc.gpsimd.tensor_scalar(slope[:], steep_sb[:], 1.0 / GROUP, 0.0, ALU.mult, ALU.add)
+        nc.gpsimd.tensor_scalar(neg_slope[:], steep_sb[:], -1.0 / GROUP, 0.0, ALU.mult, ALU.add)
+
+        wo_bf = keep.tile([P, R, PACK], BF16, name="wo_bf", align_bytes=64)
+        wo_c = keep.tile([P, R], U32, name="wo_c", align_bytes=64)
+        wo_s = keep.tile([P, R], U8, name="wo_s", align_bytes=64)
+
+        a_ps = [psum.tile([P, HALF], F32, name="a_ps%d" % h) for h in range(2)]
+        sums = keep.tile([P, G], F32, name="sums")
+        got_w = [keep.tile([P, HALF], U32, name="got_w%d" % h, align_bytes=64) for h in range(2)]
+        for h in range(2):
+            nc.vector.tensor_copy(got_w[h][:], tab_w[:].indirect(offsets[:, 16 * h : 16 * (h + 1)]))
+            nc.tensor.matmul_mx(
+                a_ps[h][:],
+                lhsT=w1_c[:].bitcast(FP8X4),
+                lhsT_scale=w1_s[:],
+                rhs=got_w[h][:].bitcast(FP8X4),
+                rhs_scale=got_s[:, h * HALF : (h + 1) * HALF],
+                start=True,
+                stop=True,
+            )
+        interleave(nc.scalar.copy, wo_bf[:], wo_raw[:])
+        nc.vector.tensor_reduce(sums[:, 0:16], by_group(a_ps[0][:]), AXIS_X, ALU.add)
+        quantize(nc, wo_c[:], wo_s[:], wo_bf[:])
+        nc.vector.tensor_reduce(sums[:, 16:32], by_group(a_ps[1][:]), AXIS_X, ALU.add)
+
+        gate = keep.tile([P, G], F32, name="gate")
+        nc.scalar.activation(gate[:], sums[:], ACT.Sigmoid, bias=bias_sb[:], scale=slope[:])
+
+        dy_bf = [keep.tile([P, QUARTER, PACK], BF16, name="dy_bf%d" % c, align_bytes=64) for c in range(4)]
+        dy_c = [keep.tile([P, QUARTER], U32, name="dy_c%d" % c, align_bytes=64) for c in range(4)]
+        dy_s = [keep.tile([P, QUARTER], U8, name="dy_s%d" % c, align_bytes=64) for c in range(4)]
+        c_ps = [psum.tile([P, QUARTER], F32, name="c_ps%d" % c) for c in range(4)]
+
+        def cast(c, copy):
+            lo = (c % 2) * QUARTER
+            interleave(copy, dy_bf[c][:], dy_raw[c // 2][:, :, lo : lo + QUARTER])
+
+        def product(c):
+            quantize(nc, dy_c[c][:], dy_s[c][:], dy_bf[c][:])
+            nc.tensor.matmul_mx(
+                c_ps[c][:],
+                lhsT=wo_c[:].bitcast(FP8X4),
+                lhsT_scale=wo_s[:],
+                rhs=dy_c[c][:].bitcast(FP8X4),
+                rhs_scale=dy_s[c][:],
+                start=True,
+                stop=True,
+            )
+
+        cast(0, nc.vector.tensor_copy)
+        cast(1, nc.scalar.copy)
+        neg_deriv = keep.tile([P, G], F32, name="neg_deriv")
+        nc.vector.scalar_tensor_tensor(neg_deriv[:], gate[:], 1.0, gate[:], ALU.subtract, ALU.mult)
+        product(0)
+        a_w = [keep.tile([P, HALF], F32, name="a_w%d" % h) for h in range(2)]
+        for h in range(2):
+            nc.vector.scalar_tensor_tensor(
+                by_group(a_w[h][:]),
+                by_group(a_ps[h][:]),
+                neg_slope[:],
+                spread(neg_deriv[:, 16 * h : 16 * (h + 1)]),
+                ALU.mult,
+                ALU.mult,
+            )
+        product(1)
+        cast(2, nc.scalar.copy)
+        cast(3, nc.scalar.copy)
+
+        def finish(c):
+            lo = (c % 2) * QUARTER
+            cols = slice(c * QUARTER, (c + 1) * QUARTER)
+            groups = slice(c * 8, (c + 1) * 8)
+            prod = keep.tile([P, QUARTER], F32, name="prod%d" % c)
+            gated = keep.tile([P, QUARTER], F32, name="gated%d" % c)
+            e1 = keep.tile([P, 8], F32, name="e1_%d" % c)
+            with_old = keep.tile([P, QUARTER], F32, name="with_old%d" % c)
+            res = keep.tile([P, QUARTER], F32, name="res%d" % c)
+            nc.vector.tensor_tensor(prod[:], c_ps[c][:], a_w[c // 2][:, lo : lo + QUARTER], ALU.mult)
+            nc.vector.tensor_tensor(by_group(gated[:]), by_group(c_ps[c][:]), spread(gate[:, groups]), ALU.mult)
+            nc.vector.tensor_reduce(e1[:], by_group(prod[:]), AXIS_X, ALU.add)
+            nc.vector.tensor_tensor(with_old[:], gated[:], old_sb[:, cols], ALU.add)
+            nc.vector.tensor_tensor(by_group(res[:]), by_group(with_old[:]), spread(e1[:]), ALU.add)
+            nc.sync.dma_start(out[:, cols], res[:])
+
+        finish(0)
+        product(2)
+        finish(1)
+        product(3)
+        finish(2)
+        finish(3)

@@ -59,25 +59,25 @@ def tile_attend_csqueeze_kernel(tc, tab_words, tab_scales, w1, steep, bias, wo, 
         old_sb = keep.tile([P, J], F32, name="old_sb")
         steep_sb = keep.tile([P, 1], F32, name="steep_sb")
         bias_sb = keep.tile([P, 1], F32, name="bias_sb")
-        warm = keep.tile([P, 1], F32, name="warm")
-        warm_out = keep.tile([P, 1], F32, name="warm_out")
 
         nc.vector.memset(tab_s[:].bitcast(I32), 0)
         nc.sync.dma_start(offsets[:], offs)
+        nc.sync.dma_start(w1_raw[:], w1.rearrange("(p t) r -> p t r", t=PACK))
         scale_rows = tab_scales[0].bitcast(I32)
         for q in (0, 2, 1, 3):
-            nc.scalar.dma_start(
+            nc.sync.dma_start(
                 tab_s[32 * q : 32 * q + 4, :].bitcast(I32), scale_rows[4 * q : 4 * q + 4, :]
             )
-        nc.vector.memset(warm[:], 0.0)
-        nc.scalar.activation(warm_out[:], warm[:], ACT.Sigmoid)
-        nc.sync.dma_start(w1_raw[:], w1.rearrange("(p t) r -> p t r", t=PACK))
         nc.sync.dma_start(
             tab_w[:].bitcast(I32), tab_words[0].rearrange("p n t -> p (n t)").bitcast(I32)
         )
-        nc.gpsimd.dma_start(steep_sb[:], steep)
-        nc.gpsimd.dma_start(bias_sb[:], bias)
         nc.sync.dma_start(wo_raw[:], wo.rearrange("(p t) r -> p t r", t=PACK))
+        nc.sync.dma_start(steep_sb[:], steep)
+        nc.sync.dma_start(bias_sb[:], bias)
+        warm = keep.tile([P, 1], F32, name="warm")
+        warm_out = keep.tile([P, 1], F32, name="warm_out")
+        nc.vector.memset(warm[:], 0.0)
+        nc.scalar.activation(warm_out[:], warm[:], ACT.Sigmoid)
         dy_planes = dy.rearrange("(p t) j -> p t j", t=PACK)
         for h in range(2):
             nc.sync.dma_start(dy_raw[h][:], dy_planes[:, :, h * HALF : (h + 1) * HALF])
@@ -89,20 +89,20 @@ def tile_attend_csqueeze_kernel(tc, tab_words, tab_scales, w1, steep, bias, wo, 
         w1_bf = keep.tile([P, R, PACK], BF16, name="w1_bf", align_bytes=64)
         w1_c = keep.tile([P, R], U32, name="w1_c", align_bytes=64)
         w1_s = keep.tile([P, R], U8, name="w1_s", align_bytes=64)
-        interleave(nc.scalar.copy, w1_bf[:], w1_raw[:])
+        interleave(nc.vector.tensor_copy, w1_bf[:], w1_raw[:])
         quantize(nc, w1_c[:], w1_s[:], w1_bf[:])
 
         slope = keep.tile([P, 1], F32, name="slope")
+        nc.scalar.activation(slope[:], steep_sb[:], ACT.Copy, scale=1.0 / GROUP)
         neg_slope = keep.tile([P, 1], F32, name="neg_slope")
-        nc.gpsimd.tensor_scalar(slope[:], steep_sb[:], 1.0 / GROUP, 0.0, ALU.mult, ALU.add)
-        nc.gpsimd.tensor_scalar(neg_slope[:], steep_sb[:], -1.0 / GROUP, 0.0, ALU.mult, ALU.add)
+        nc.scalar.activation(neg_slope[:], steep_sb[:], ACT.Copy, scale=-1.0 / GROUP)
 
         wo_bf = keep.tile([P, R, PACK], BF16, name="wo_bf", align_bytes=64)
         wo_c = keep.tile([P, R], U32, name="wo_c", align_bytes=64)
         wo_s = keep.tile([P, R], U8, name="wo_s", align_bytes=64)
 
         a_ps = [psum.tile([P, HALF], F32, name="a_ps%d" % h) for h in range(2)]
-        sums = keep.tile([P, G], F32, name="sums")
+        sums = [keep.tile([P, 16], F32, name="sums%d" % h) for h in range(2)]
         got_w = [keep.tile([P, HALF], U32, name="got_w%d" % h, align_bytes=64) for h in range(2)]
         for h in range(2):
             nc.vector.tensor_copy(got_w[h][:], tab_w[:].indirect(offsets[:, 16 * h : 16 * (h + 1)]))
@@ -116,12 +116,12 @@ def tile_attend_csqueeze_kernel(tc, tab_words, tab_scales, w1, steep, bias, wo, 
                 stop=True,
             )
         interleave(nc.scalar.copy, wo_bf[:], wo_raw[:])
-        nc.vector.tensor_reduce(sums[:, 0:16], by_group(a_ps[0][:]), AXIS_X, ALU.add)
         quantize(nc, wo_c[:], wo_s[:], wo_bf[:])
-        nc.vector.tensor_reduce(sums[:, 16:32], by_group(a_ps[1][:]), AXIS_X, ALU.add)
+        gate = [keep.tile([P, 16], F32, name="gate%d" % h) for h in range(2)]
 
-        gate = keep.tile([P, G], F32, name="gate")
-        nc.scalar.activation(gate[:], sums[:], ACT.Sigmoid, bias=bias_sb[:], scale=slope[:])
+        def make_gate(h):
+            nc.vector.tensor_reduce(sums[h][:], by_group(a_ps[h][:]), AXIS_X, ALU.add)
+            nc.scalar.activation(gate[h][:], sums[h][:], ACT.Sigmoid, bias=bias_sb[:], scale=slope[:])
 
         dy_bf = [keep.tile([P, QUARTER, PACK], BF16, name="dy_bf%d" % c, align_bytes=64) for c in range(4)]
         dy_c = [keep.tile([P, QUARTER], U32, name="dy_c%d" % c, align_bytes=64) for c in range(4)]
@@ -144,44 +144,56 @@ def tile_attend_csqueeze_kernel(tc, tab_words, tab_scales, w1, steep, bias, wo, 
                 stop=True,
             )
 
+        def tiles(stem, width):
+            return [keep.tile([P, width], F32, name="%s%d" % (stem, c))[:] for c in range(4)]
+
+        gated, prod, with_old, res = (tiles(stem, QUARTER) for stem in ("gated", "prod", "with_old", "res"))
+        dots, e1 = tiles("dots", 8), tiles("e1_", 8)
+        for c in range(2):
+            prod[c] = dy_raw[1][:, c, 0:QUARTER]
+            dots[c] = dy_raw[1][:, c, QUARTER : QUARTER + 8]
+
+        def gate_of(c):
+            return gate[c // 2][:, (c % 2) * 8 : (c % 2 + 1) * 8]
+
+        def step_gate(c):
+            nc.vector.tensor_tensor(by_group(gated[c]), by_group(c_ps[c][:]), spread(gate_of(c)), ALU.mult)
+            nc.gpsimd.tensor_tensor(with_old[c], gated[c], old_sb[:, c * QUARTER : (c + 1) * QUARTER], ALU.add)
+
+        def step_prod(c):
+            lo = (c % 2) * QUARTER
+            nc.vector.scalar_tensor_tensor(
+                prod[c], gated[c], neg_slope[:], a_ps[c // 2][:, lo : lo + QUARTER], ALU.mult, ALU.mult
+            )
+
+        def step_dots(c):
+            nc.vector.tensor_reduce(dots[c], by_group(prod[c]), AXIS_X, ALU.add)
+
+        def step_e1(c):
+            nc.vector.scalar_tensor_tensor(e1[c], gate_of(c), 1.0, dots[c], ALU.subtract, ALU.mult)
+
+        def step_res(c):
+            if c < 2:
+                for g in range(8):
+                    cols = slice(g * GROUP, (g + 1) * GROUP)
+                    nc.scalar.activation(res[c][:, cols], with_old[c][:, cols], ACT.Identity, bias=e1[c][:, g : g + 1])
+            else:
+                nc.vector.tensor_tensor(by_group(res[c]), by_group(with_old[c]), spread(e1[c]), ALU.add)
+            nc.sync.dma_start(out[:, c * QUARTER : (c + 1) * QUARTER], res[c])
+
+        make_gate(0)
         cast(0, nc.vector.tensor_copy)
         cast(1, nc.scalar.copy)
-        neg_deriv = keep.tile([P, G], F32, name="neg_deriv")
-        nc.vector.scalar_tensor_tensor(neg_deriv[:], gate[:], 1.0, gate[:], ALU.subtract, ALU.mult)
         product(0)
-        a_w = [keep.tile([P, HALF], F32, name="a_w%d" % h) for h in range(2)]
-        for h in range(2):
-            nc.vector.scalar_tensor_tensor(
-                by_group(a_w[h][:]),
-                by_group(a_ps[h][:]),
-                neg_slope[:],
-                spread(neg_deriv[:, 16 * h : 16 * (h + 1)]),
-                ALU.mult,
-                ALU.mult,
-            )
+        make_gate(1)
         product(1)
         cast(2, nc.scalar.copy)
         cast(3, nc.scalar.copy)
-
-        def finish(c):
-            lo = (c % 2) * QUARTER
-            cols = slice(c * QUARTER, (c + 1) * QUARTER)
-            groups = slice(c * 8, (c + 1) * 8)
-            prod = keep.tile([P, QUARTER], F32, name="prod%d" % c)
-            gated = keep.tile([P, QUARTER], F32, name="gated%d" % c)
-            e1 = keep.tile([P, 8], F32, name="e1_%d" % c)
-            with_old = keep.tile([P, QUARTER], F32, name="with_old%d" % c)
-            res = keep.tile([P, QUARTER], F32, name="res%d" % c)
-            nc.vector.tensor_tensor(prod[:], c_ps[c][:], a_w[c // 2][:, lo : lo + QUARTER], ALU.mult)
-            nc.vector.tensor_tensor(by_group(gated[:]), by_group(c_ps[c][:]), spread(gate[:, groups]), ALU.mult)
-            nc.vector.tensor_reduce(e1[:], by_group(prod[:]), AXIS_X, ALU.add)
-            nc.vector.tensor_tensor(with_old[:], gated[:], old_sb[:, cols], ALU.add)
-            nc.vector.tensor_tensor(by_group(res[:]), by_group(with_old[:]), spread(e1[:]), ALU.add)
-            nc.sync.dma_start(out[:, cols], res[:])
-
-        finish(0)
         product(2)
-        finish(1)
         product(3)
-        finish(2)
-        finish(3)
+        steps = (step_gate, step_prod, step_dots, step_e1, step_res)
+        for wave in range(len(steps) + 2):
+            for half in range(2):
+                for lag, first in ((2, 2), (0, 0)):
+                    if 0 <= wave - lag < len(steps):
+                        steps[wave - lag](first + half)

@@ -61,8 +61,8 @@ def tile_attend_csqueeze_kernel(tc, tab_words, tab_scales, w1, steep, bias, wo, 
         bias_sb = keep.tile([P, 1], F32, name="bias_sb")
 
         nc.vector.memset(tab_s[:].bitcast(I32), 0)
-        nc.sync.dma_start(offsets[:], offs)
         nc.sync.dma_start(w1_raw[:], w1.rearrange("(p t) r -> p t r", t=PACK))
+        nc.sync.dma_start(offsets[:], offs)
         scale_rows = tab_scales[0].bitcast(I32)
         for q in (0, 2, 1, 3):
             nc.sync.dma_start(
@@ -117,62 +117,71 @@ def tile_attend_csqueeze_kernel(tc, tab_words, tab_scales, w1, steep, bias, wo, 
             )
         interleave(nc.scalar.copy, wo_bf[:], wo_raw[:])
         quantize(nc, wo_c[:], wo_s[:], wo_bf[:])
-        gate = [keep.tile([P, 16], F32, name="gate%d" % h) for h in range(2)]
+        gate = [keep.tile([P, 16], F32, name="gate0")[:], dy_raw[0][:, 0, QUARTER : QUARTER + 16]]
+        neg_deriv = [keep.tile([P, 16], F32, name="neg_deriv%d" % h)[:] for h in range(2)]
+
+        def group_sums(h):
+            nc.vector.tensor_reduce(sums[h][:], by_group(a_ps[h][:]), AXIS_X, ALU.add)
 
         def make_gate(h):
-            nc.vector.tensor_reduce(sums[h][:], by_group(a_ps[h][:]), AXIS_X, ALU.add)
-            nc.scalar.activation(gate[h][:], sums[h][:], ACT.Sigmoid, bias=bias_sb[:], scale=slope[:])
+            nc.scalar.activation(gate[h], sums[h][:], ACT.Sigmoid, bias=bias_sb[:], scale=slope[:])
 
-        dy_bf = [keep.tile([P, QUARTER, PACK], BF16, name="dy_bf%d" % c, align_bytes=64) for c in range(4)]
-        dy_c = [keep.tile([P, QUARTER], U32, name="dy_c%d" % c, align_bytes=64) for c in range(4)]
-        dy_s = [keep.tile([P, QUARTER], U8, name="dy_s%d" % c, align_bytes=64) for c in range(4)]
-        c_ps = [psum.tile([P, QUARTER], F32, name="c_ps%d" % c) for c in range(4)]
+        def derivative(h):
+            nc.vector.scalar_tensor_tensor(neg_deriv[h], gate[h], 1.0, gate[h], ALU.subtract, ALU.mult)
 
-        def cast(c, copy):
+        def weigh(c):
             lo = (c % 2) * QUARTER
-            interleave(copy, dy_bf[c][:], dy_raw[c // 2][:, :, lo : lo + QUARTER])
+            nc.vector.scalar_tensor_tensor(
+                by_group(a_w[c]),
+                by_group(a_ps[c // 2][:, lo : lo + QUARTER]),
+                neg_slope[:],
+                spread(neg_deriv[c // 2][:, (c % 2) * 8 : (c % 2 + 1) * 8]),
+                ALU.mult,
+                ALU.mult,
+            )
+
+        def tiles(stem, shape, dtype):
+            return [keep.tile(shape, dtype, name="%s%d" % (stem, c), align_bytes=64)[:] for c in range(4)]
+
+        dy_bf = tiles("dy_bf", [P, QUARTER, PACK], BF16)
+        dy_c, dy_s = tiles("dy_c", [P, QUARTER], U32), tiles("dy_s", [P, QUARTER], U8)
+        c_ps = [psum.tile([P, QUARTER], F32, name="c_ps%d" % c)[:] for c in range(4)]
+        gated, prod, with_old, res = (
+            tiles(stem, [P, QUARTER], F32) for stem in ("gated", "prod", "with_old", "res")
+        )
+        e1 = tiles("e1_", [P, 8], F32)
+        a_w = [dy_raw[0][:, 0, 0:QUARTER], dy_raw[0][:, 1, 0:QUARTER]] + tiles("a_w", [P, QUARTER], F32)[2:]
+        prod[1], gated[1] = dy_raw[1][:, 0, 0:QUARTER], dy_raw[1][:, 1, 0:QUARTER]
+        e1[0] = dy_raw[1][:, 2, 0:8]
+
+        def cast(c, lo, hi, copy):
+            start = (c % 2) * QUARTER
+            interleave(copy, dy_bf[c][:, lo:hi, :], dy_raw[c // 2][:, :, start + lo : start + hi])
 
         def product(c):
-            quantize(nc, dy_c[c][:], dy_s[c][:], dy_bf[c][:])
+            quantize(nc, dy_c[c], dy_s[c], dy_bf[c])
             nc.tensor.matmul_mx(
-                c_ps[c][:],
+                c_ps[c],
                 lhsT=wo_c[:].bitcast(FP8X4),
                 lhsT_scale=wo_s[:],
-                rhs=dy_c[c][:].bitcast(FP8X4),
-                rhs_scale=dy_s[c][:],
+                rhs=dy_c[c].bitcast(FP8X4),
+                rhs_scale=dy_s[c],
                 start=True,
                 stop=True,
             )
 
-        def tiles(stem, width):
-            return [keep.tile([P, width], F32, name="%s%d" % (stem, c))[:] for c in range(4)]
+        def multiply(c):
+            nc.vector.tensor_tensor(prod[c], c_ps[c], a_w[c], ALU.mult)
+            gate_c = gate[c // 2][:, (c % 2) * 8 : (c % 2 + 1) * 8]
+            nc.vector.tensor_tensor(by_group(gated[c]), by_group(c_ps[c]), spread(gate_c), ALU.mult)
 
-        gated, prod, with_old, res = (tiles(stem, QUARTER) for stem in ("gated", "prod", "with_old", "res"))
-        dots, e1 = tiles("dots", 8), tiles("e1_", 8)
-        for c in range(2):
-            prod[c] = dy_raw[1][:, c, 0:QUARTER]
-            dots[c] = dy_raw[1][:, c, QUARTER : QUARTER + 8]
+        def group_dots(c):
+            nc.vector.tensor_reduce(e1[c], by_group(prod[c]), AXIS_X, ALU.add)
 
-        def gate_of(c):
-            return gate[c // 2][:, (c % 2) * 8 : (c % 2 + 1) * 8]
+        def add_old(c, engine):
+            engine.tensor_tensor(with_old[c], gated[c], old_sb[:, c * QUARTER : (c + 1) * QUARTER], ALU.add)
 
-        def step_gate(c):
-            nc.vector.tensor_tensor(by_group(gated[c]), by_group(c_ps[c][:]), spread(gate_of(c)), ALU.mult)
-            nc.gpsimd.tensor_tensor(with_old[c], gated[c], old_sb[:, c * QUARTER : (c + 1) * QUARTER], ALU.add)
-
-        def step_prod(c):
-            lo = (c % 2) * QUARTER
-            nc.vector.scalar_tensor_tensor(
-                prod[c], gated[c], neg_slope[:], a_ps[c // 2][:, lo : lo + QUARTER], ALU.mult, ALU.mult
-            )
-
-        def step_dots(c):
-            nc.vector.tensor_reduce(dots[c], by_group(prod[c]), AXIS_X, ALU.add)
-
-        def step_e1(c):
-            nc.vector.scalar_tensor_tensor(e1[c], gate_of(c), 1.0, dots[c], ALU.subtract, ALU.mult)
-
-        def step_res(c):
+        def finish(c):
             if c < 2:
                 for g in range(8):
                     cols = slice(g * GROUP, (g + 1) * GROUP)
@@ -181,19 +190,37 @@ def tile_attend_csqueeze_kernel(tc, tab_words, tab_scales, w1, steep, bias, wo, 
                 nc.vector.tensor_tensor(by_group(res[c]), by_group(with_old[c]), spread(e1[c]), ALU.add)
             nc.sync.dma_start(out[:, c * QUARTER : (c + 1) * QUARTER], res[c])
 
+        group_sums(0)
         make_gate(0)
-        cast(0, nc.vector.tensor_copy)
-        cast(1, nc.scalar.copy)
-        product(0)
+        group_sums(1)
+        derivative(0)
+        cast(0, 0, QUARTER, nc.vector.tensor_copy)
+        cast(1, 0, QUARTER, nc.scalar.copy)
         make_gate(1)
+        product(0)
+        weigh(0)
         product(1)
-        cast(2, nc.scalar.copy)
-        cast(3, nc.scalar.copy)
+        weigh(1)
+        derivative(1)
+        cast(2, 0, QUARTER, nc.scalar.copy)
+        cast(3, 0, 64, nc.scalar.copy)
+        weigh(2)
+        multiply(0)
+        add_old(0, nc.gpsimd)
+        weigh(3)
+        cast(3, 64, QUARTER, nc.vector.tensor_copy)
         product(2)
         product(3)
-        steps = (step_gate, step_prod, step_dots, step_e1, step_res)
-        for wave in range(len(steps) + 2):
-            for half in range(2):
-                for lag, first in ((2, 2), (0, 0)):
-                    if 0 <= wave - lag < len(steps):
-                        steps[wave - lag](first + half)
+        multiply(1)
+        add_old(1, nc.gpsimd)
+        for c in range(2):
+            group_dots(c)
+            finish(c)
+        multiply(2)
+        add_old(2, nc.gpsimd)
+        multiply(3)
+        group_dots(2)
+        group_dots(3)
+        add_old(3, nc.vector)
+        finish(2)
+        finish(3)

@@ -74,10 +74,6 @@ def tile_attend_csqueeze_kernel(tc, tab_words, tab_scales, w1, steep, bias, wo, 
         nc.sync.dma_start(wo_raw[:], wo.rearrange("(p t) r -> p t r", t=PACK))
         nc.sync.dma_start(steep_sb[:], steep)
         nc.sync.dma_start(bias_sb[:], bias)
-        warm = keep.tile([P, 1], F32, name="warm")
-        warm_out = keep.tile([P, 1], F32, name="warm_out")
-        nc.vector.memset(warm[:], 0.0)
-        nc.scalar.activation(warm_out[:], warm[:], ACT.Sigmoid)
         dy_planes = dy.rearrange("(p t) j -> p t j", t=PACK)
         for h in range(2):
             nc.sync.dma_start(dy_raw[h][:], dy_planes[:, :, h * HALF : (h + 1) * HALF])

@@ -18,21 +18,40 @@ AXIS_X = mybir.AxisListType.X
 
 P = 128
 PACK = 4
+QUADRANT = 32
+LINE = 4
+PER_COLUMN = 16
 GROUP = J // G
 HALF = J // 2
 QUARTER = J // 4
+HALF_GROUPS = HALF // GROUP
+QUARTER_GROUPS = QUARTER // GROUP
+ALIGN = 64
+LAST_SPLIT = QUARTER // 2
 
 
 def interleave(copy, grouped, raw):
     copy(
-        out=grouped.rearrange("p (c i) t -> p c t i", i=4),
-        in_=raw.rearrange("p t (c i) -> p c t i", i=4),
+        out=grouped.rearrange("p (line i) t -> p line t i", i=LINE),
+        in_=raw.rearrange("p t (line i) -> p line t i", i=LINE),
     )
 
 
 def quantize(nc, codes, scales, grouped):
     nc.vector.quantize_mx(
         out=codes.bitcast(FP8X4), scales=scales, in_=grouped.rearrange("p w t -> p (w t)")
+    )
+
+
+def one_pass(nc, result, weight_codes, weight_scales, codes, scales):
+    nc.tensor.matmul_mx(
+        result,
+        lhsT=weight_codes.bitcast(FP8X4),
+        lhsT_scale=weight_scales,
+        rhs=codes.bitcast(FP8X4),
+        rhs_scale=scales,
+        start=True,
+        stop=True,
     )
 
 
@@ -44,179 +63,169 @@ def spread(ap):
     return ap.unsqueeze(2).to_broadcast([P, ap.shape[1], GROUP])
 
 
+def groups_of(ap, qt):
+    return ap[:, qt * QUARTER_GROUPS : (qt + 1) * QUARTER_GROUPS]
+
+
 def tile_attend_csqueeze_kernel(tc, tab_words, tab_scales, w1, steep, bias, wo, dy, old, offs, out):
     nc = tc.nc
     with ExitStack() as ctx:
         keep = ctx.enter_context(tc.tile_pool(name="keep", bufs=1))
         psum = ctx.enter_context(tc.psum_pool(name="psum", bufs=1))
 
-        offsets = keep.tile([P, J // 16], U16, name="offsets")
-        tab_s = keep.tile([P, T], U8, name="tab_s", align_bytes=64)
-        tab_w = keep.tile([P, T], U32, name="tab_w", align_bytes=64)
-        w1_raw = keep.tile([P, PACK, R], F32, name="w1_raw")
-        wo_raw = keep.tile([P, PACK, R], F32, name="wo_raw")
-        dy_raw = [keep.tile([P, PACK, HALF], F32, name="dy_raw%d" % h) for h in range(2)]
-        old_sb = keep.tile([P, J], F32, name="old_sb")
-        steep_sb = keep.tile([P, 1], F32, name="steep_sb")
-        bias_sb = keep.tile([P, 1], F32, name="bias_sb")
+        def new_tile(name, shape, dtype):
+            return keep.tile(shape, dtype, name=name, align_bytes=ALIGN)[:]
 
-        nc.vector.memset(tab_s[:].bitcast(I32), 0)
-        nc.sync.dma_start(w1_raw[:], w1.rearrange("(p t) r -> p t r", t=PACK))
+        def new_tiles(stem, shape, dtype, count):
+            return [new_tile("%s%d" % (stem, n), shape, dtype) for n in range(count)]
+
+        offsets = keep.tile([P, J // PER_COLUMN], U16, name="offsets")
+        tab_s = new_tile("tab_s", [P, T], U8)
+        tab_w = new_tile("tab_w", [P, T], U32)
+        w1_raw = new_tile("w1_raw", [P, PACK, R], F32)
+        wo_raw = new_tile("wo_raw", [P, PACK, R], F32)
+        dy_raw = new_tiles("dy_raw", [P, PACK, HALF], F32, 2)
+        old_sb = new_tile("old_sb", [P, J], F32)
+        rows = new_tile("rows", [P, QUADRANT], F32)
+
+        nc.vector.memset(tab_s.bitcast(I32), 0)
+        nc.vector.memset(rows, 0.0)
+        nc.sync.dma_start(w1_raw, w1.rearrange("(p t) r -> p t r", t=PACK))
         nc.sync.dma_start(offsets[:], offs)
         scale_rows = tab_scales[0].bitcast(I32)
         for q in (0, 2, 1, 3):
             nc.sync.dma_start(
-                tab_s[32 * q : 32 * q + 4, :].bitcast(I32), scale_rows[4 * q : 4 * q + 4, :]
+                tab_s[QUADRANT * q : QUADRANT * q + 4, :].bitcast(I32), scale_rows[4 * q : 4 * q + 4, :]
             )
-        nc.sync.dma_start(
-            tab_w[:].bitcast(I32), tab_words[0].rearrange("p n t -> p (n t)").bitcast(I32)
-        )
-        nc.sync.dma_start(wo_raw[:], wo.rearrange("(p t) r -> p t r", t=PACK))
-        nc.sync.dma_start(steep_sb[:], steep)
-        nc.sync.dma_start(bias_sb[:], bias)
+        nc.sync.dma_start(tab_w.bitcast(I32), tab_words[0].rearrange("p n t -> p (n t)").bitcast(I32))
+        nc.sync.dma_start(wo_raw, wo.rearrange("(p t) r -> p t r", t=PACK))
+        nc.sync.dma_start(rows[0:P:QUADRANT, :], steep.rearrange("(q i) o -> q (i o)", i=QUADRANT))
+        nc.sync.dma_start(rows[1:P:QUADRANT, :], bias.rearrange("(q i) o -> q (i o)", i=QUADRANT))
+        warm = new_tile("warm", [P, 1], F32)
+        warm_out = new_tile("warm_out", [P, 1], F32)
+        nc.vector.memset(warm, 0.0)
+        nc.scalar.activation(warm_out, warm, ACT.Sigmoid)
         dy_planes = dy.rearrange("(p t) j -> p t j", t=PACK)
         for h in range(2):
-            nc.sync.dma_start(dy_raw[h][:], dy_planes[:, :, h * HALF : (h + 1) * HALF])
-        nc.sync.dma_start(old_sb[:], old)
+            nc.sync.dma_start(dy_raw[h], dy_planes[:, :, h * HALF : (h + 1) * HALF])
+        nc.sync.dma_start(old_sb, old)
 
-        got_s = keep.tile([P, J], U8, name="got_s", align_bytes=64)
-        nc.vector.tensor_copy(got_s[:], tab_s[:].indirect(offsets[:]))
+        got_s = new_tile("got_s", [P, J], U8)
+        nc.vector.tensor_copy(got_s, tab_s.indirect(offsets[:]))
 
-        w1_bf = keep.tile([P, R, PACK], BF16, name="w1_bf", align_bytes=64)
-        w1_c = keep.tile([P, R], U32, name="w1_c", align_bytes=64)
-        w1_s = keep.tile([P, R], U8, name="w1_s", align_bytes=64)
-        interleave(nc.vector.tensor_copy, w1_bf[:], w1_raw[:])
-        quantize(nc, w1_c[:], w1_s[:], w1_bf[:])
+        w1_bf = new_tile("w1_bf", [P, R, PACK], BF16)
+        w1_c, w1_s = new_tile("w1_c", [P, R], U32), new_tile("w1_s", [P, R], U8)
+        interleave(nc.vector.tensor_copy, w1_bf, w1_raw)
+        quantize(nc, w1_c, w1_s, w1_bf)
 
-        slope = keep.tile([P, 1], F32, name="slope")
-        nc.scalar.activation(slope[:], steep_sb[:], ACT.Copy, scale=1.0 / GROUP)
-        neg_slope = keep.tile([P, 1], F32, name="neg_slope")
-        nc.scalar.activation(neg_slope[:], steep_sb[:], ACT.Copy, scale=-1.0 / GROUP)
-
-        wo_bf = keep.tile([P, R, PACK], BF16, name="wo_bf", align_bytes=64)
-        wo_c = keep.tile([P, R], U32, name="wo_c", align_bytes=64)
-        wo_s = keep.tile([P, R], U8, name="wo_s", align_bytes=64)
-
-        a_ps = [psum.tile([P, HALF], F32, name="a_ps%d" % h) for h in range(2)]
-        sums = [keep.tile([P, 16], F32, name="sums%d" % h) for h in range(2)]
-        got_w = [keep.tile([P, HALF], U32, name="got_w%d" % h, align_bytes=64) for h in range(2)]
+        a_ps = [psum.tile([P, HALF], F32, name="a_ps%d" % h)[:] for h in range(2)]
+        got_w = new_tiles("got_w", [P, HALF], U32, 2)
+        half_columns = HALF // PER_COLUMN
         for h in range(2):
-            nc.vector.tensor_copy(got_w[h][:], tab_w[:].indirect(offsets[:, 16 * h : 16 * (h + 1)]))
-            nc.tensor.matmul_mx(
-                a_ps[h][:],
-                lhsT=w1_c[:].bitcast(FP8X4),
-                lhsT_scale=w1_s[:],
-                rhs=got_w[h][:].bitcast(FP8X4),
-                rhs_scale=got_s[:, h * HALF : (h + 1) * HALF],
-                start=True,
-                stop=True,
-            )
-        interleave(nc.scalar.copy, wo_bf[:], wo_raw[:])
-        quantize(nc, wo_c[:], wo_s[:], wo_bf[:])
-        gate = [keep.tile([P, 16], F32, name="gate0")[:], dy_raw[0][:, 0, QUARTER : QUARTER + 16]]
-        neg_deriv = [keep.tile([P, 16], F32, name="neg_deriv%d" % h)[:] for h in range(2)]
+            half_offsets = offsets[:, h * half_columns : (h + 1) * half_columns]
+            nc.vector.tensor_copy(got_w[h], tab_w.indirect(half_offsets))
+            one_pass(nc, a_ps[h], w1_c, w1_s, got_w[h], got_s[:, h * HALF : (h + 1) * HALF])
 
-        def group_sums(h):
-            nc.vector.tensor_reduce(sums[h][:], by_group(a_ps[h][:]), AXIS_X, ALU.add)
+        wo_bf = new_tile("wo_bf", [P, R, PACK], BF16)
+        wo_c, wo_s = new_tile("wo_c", [P, R], U32), new_tile("wo_s", [P, R], U8)
+        interleave(nc.scalar.copy, wo_bf, wo_raw)
+        quantize(nc, wo_c, wo_s, wo_bf)
 
-        def make_gate(h):
-            nc.scalar.activation(gate[h], sums[h][:], ACT.Sigmoid, bias=bias_sb[:], scale=slope[:])
+        columns = new_tile("columns", [P, QUADRANT], F32)
+        slope = new_tile("slope", [P, 1], F32)
+        nc.vector.transpose(columns, rows)
+        nc.gpsimd.tensor_scalar(slope, columns[:, 0:1], 1.0 / GROUP, 0.0, ALU.mult, ALU.add)
 
-        def derivative(h):
-            nc.vector.scalar_tensor_tensor(neg_deriv[h], gate[h], 1.0, gate[h], ALU.subtract, ALU.mult)
+        dy_bf = new_tiles("dy_bf", [P, QUARTER, PACK], BF16, 4)
+        dy_c, dy_s = new_tiles("dy_c", [P, QUARTER], U32, 4), new_tiles("dy_s", [P, QUARTER], U8, 4)
+        c0_ps = [psum.tile([P, QUARTER], F32, name="c0_ps%d" % qt)[:] for qt in range(4)]
+        sums, neg_deriv = new_tile("sums", [P, G], F32), new_tile("neg_deriv", [P, G], F32)
+        neg_a_w = new_tiles("neg_a_w", [P, QUARTER], F32, 4)
+        with_old, res = new_tiles("with_old", [P, QUARTER], F32, 4), new_tiles("res", [P, QUARTER], F32, 4)
 
-        def weigh(c):
-            lo = (c % 2) * QUARTER
+        def freed(qt, t, width):
+            first = (qt % 2) * QUARTER
+            return dy_raw[qt // 2][:, t, first : first + width]
+
+        gate = freed(1, 0, G)
+        prod = [freed(2, 0, QUARTER) if qt == 1 else new_tile("prod%d" % qt, [P, QUARTER], F32) for qt in range(4)]
+        gated = [freed(2, 1, QUARTER) if qt == 1 else new_tile("gated%d" % qt, [P, QUARTER], F32) for qt in range(4)]
+        e1 = [freed(2, 2, QUARTER_GROUPS)] + new_tiles("e1_", [P, QUARTER_GROUPS], F32, 3)
+
+        def weigh(qt):
+            first = (qt % 2) * QUARTER
             nc.vector.scalar_tensor_tensor(
-                by_group(a_w[c]),
-                by_group(a_ps[c // 2][:, lo : lo + QUARTER]),
-                neg_slope[:],
-                spread(neg_deriv[c // 2][:, (c % 2) * 8 : (c % 2 + 1) * 8]),
+                by_group(neg_a_w[qt]),
+                by_group(a_ps[qt // 2][:, first : first + QUARTER]),
+                slope,
+                spread(groups_of(neg_deriv, qt)),
                 ALU.mult,
                 ALU.mult,
             )
 
-        def tiles(stem, shape, dtype):
-            return [keep.tile(shape, dtype, name="%s%d" % (stem, c), align_bytes=64)[:] for c in range(4)]
+        def round_dy(qt, lo, hi, copy):
+            first = (qt % 2) * QUARTER
+            interleave(copy, dy_bf[qt][:, lo:hi, :], dy_raw[qt // 2][:, :, first + lo : first + hi])
 
-        dy_bf = tiles("dy_bf", [P, QUARTER, PACK], BF16)
-        dy_c, dy_s = tiles("dy_c", [P, QUARTER], U32), tiles("dy_s", [P, QUARTER], U8)
-        c_ps = [psum.tile([P, QUARTER], F32, name="c_ps%d" % c)[:] for c in range(4)]
-        gated, prod, with_old, res = (
-            tiles(stem, [P, QUARTER], F32) for stem in ("gated", "prod", "with_old", "res")
-        )
-        e1 = tiles("e1_", [P, 8], F32)
-        a_w = [dy_raw[0][:, 0, 0:QUARTER], dy_raw[0][:, 1, 0:QUARTER]] + tiles("a_w", [P, QUARTER], F32)[2:]
-        prod[1], gated[1] = dy_raw[1][:, 0, 0:QUARTER], dy_raw[1][:, 1, 0:QUARTER]
-        e1[0] = dy_raw[1][:, 2, 0:8]
+        def second_product(qt):
+            quantize(nc, dy_c[qt], dy_s[qt], dy_bf[qt])
+            one_pass(nc, c0_ps[qt], wo_c, wo_s, dy_c[qt], dy_s[qt])
 
-        def cast(c, lo, hi, copy):
-            start = (c % 2) * QUARTER
-            interleave(copy, dy_bf[c][:, lo:hi, :], dy_raw[c // 2][:, :, start + lo : start + hi])
+        def multiply(qt):
+            nc.vector.tensor_tensor(prod[qt], c0_ps[qt], neg_a_w[qt], ALU.mult)
+            nc.vector.tensor_tensor(by_group(gated[qt]), by_group(c0_ps[qt]), spread(groups_of(gate, qt)), ALU.mult)
 
-        def product(c):
-            quantize(nc, dy_c[c], dy_s[c], dy_bf[c])
-            nc.tensor.matmul_mx(
-                c_ps[c],
-                lhsT=wo_c[:].bitcast(FP8X4),
-                lhsT_scale=wo_s[:],
-                rhs=dy_c[c].bitcast(FP8X4),
-                rhs_scale=dy_s[c],
-                start=True,
-                stop=True,
-            )
+        def group_dots(qt):
+            nc.vector.tensor_reduce(e1[qt], by_group(prod[qt]), AXIS_X, ALU.add, negate=True)
 
-        def multiply(c):
-            nc.vector.tensor_tensor(prod[c], c_ps[c], a_w[c], ALU.mult)
-            gate_c = gate[c // 2][:, (c % 2) * 8 : (c % 2 + 1) * 8]
-            nc.vector.tensor_tensor(by_group(gated[c]), by_group(c_ps[c]), spread(gate_c), ALU.mult)
+        def add_old(qt, engine):
+            engine.tensor_tensor(with_old[qt], gated[qt], old_sb[:, qt * QUARTER : (qt + 1) * QUARTER], ALU.add)
 
-        def group_dots(c):
-            nc.vector.tensor_reduce(e1[c], by_group(prod[c]), AXIS_X, ALU.add)
+        def store(qt):
+            nc.sync.dma_start(out[:, qt * QUARTER : (qt + 1) * QUARTER], res[qt])
 
-        def add_old(c, engine):
-            engine.tensor_tensor(with_old[c], gated[c], old_sb[:, c * QUARTER : (c + 1) * QUARTER], ALU.add)
+        def finish_on_scalar(qt):
+            for g in range(QUARTER_GROUPS):
+                cols = slice(g * GROUP, (g + 1) * GROUP)
+                nc.scalar.activation(res[qt][:, cols], with_old[qt][:, cols], ACT.Identity, bias=e1[qt][:, g : g + 1])
+            store(qt)
 
-        def finish(c):
-            if c < 2:
-                for g in range(8):
-                    cols = slice(g * GROUP, (g + 1) * GROUP)
-                    nc.scalar.activation(res[c][:, cols], with_old[c][:, cols], ACT.Identity, bias=e1[c][:, g : g + 1])
-            else:
-                nc.vector.tensor_tensor(by_group(res[c]), by_group(with_old[c]), spread(e1[c]), ALU.add)
-            nc.sync.dma_start(out[:, c * QUARTER : (c + 1) * QUARTER], res[c])
+        def finish_on_vector(qt):
+            nc.vector.tensor_tensor(by_group(res[qt]), by_group(with_old[qt]), spread(e1[qt]), ALU.add)
+            store(qt)
 
-        group_sums(0)
-        make_gate(0)
-        group_sums(1)
-        derivative(0)
-        cast(0, 0, QUARTER, nc.vector.tensor_copy)
-        cast(1, 0, QUARTER, nc.scalar.copy)
-        make_gate(1)
-        product(0)
+        for h in range(2):
+            half_sums = sums[:, h * HALF_GROUPS : (h + 1) * HALF_GROUPS]
+            nc.vector.tensor_reduce(half_sums, by_group(a_ps[h]), AXIS_X, ALU.add)
+        round_dy(0, 0, QUARTER, nc.vector.tensor_copy)
+        round_dy(1, 0, QUARTER, nc.scalar.copy)
+        nc.scalar.activation(gate, sums, ACT.Sigmoid, bias=columns[:, 1:2], scale=slope)
+        second_product(0)
+        second_product(1)
+        nc.vector.scalar_tensor_tensor(neg_deriv, gate, 1.0, gate, ALU.subtract, ALU.mult)
         weigh(0)
-        product(1)
         weigh(1)
-        derivative(1)
-        cast(2, 0, QUARTER, nc.scalar.copy)
-        cast(3, 0, 64, nc.scalar.copy)
-        weigh(2)
+
+        round_dy(2, 0, QUARTER, nc.scalar.copy)
+        round_dy(3, 0, LAST_SPLIT, nc.scalar.copy)
         multiply(0)
         add_old(0, nc.gpsimd)
+        round_dy(3, LAST_SPLIT, QUARTER, nc.vector.tensor_copy)
+        weigh(2)
         weigh(3)
-        cast(3, 64, QUARTER, nc.vector.tensor_copy)
-        product(2)
-        product(3)
+        second_product(2)
+        second_product(3)
         multiply(1)
         add_old(1, nc.gpsimd)
-        for c in range(2):
-            group_dots(c)
-            finish(c)
+        for qt in range(2):
+            group_dots(qt)
+            finish_on_scalar(qt)
+
         multiply(2)
         add_old(2, nc.gpsimd)
         multiply(3)
         group_dots(2)
         group_dots(3)
         add_old(3, nc.vector)
-        finish(2)
-        finish(3)
+        finish_on_vector(2)
+        finish_on_vector(3)

from contextlib import ExitStack

import concourse.mybir as mybir

K, R, F, T, J, G = 512, 128, 512, 2048, 512, 32
FLOPS = 2 * K * R * J + 2 * F * R * J

F32 = mybir.dt.float32
BF16 = mybir.dt.bfloat16
I32 = mybir.dt.int32
U32 = mybir.dt.uint32
U16 = mybir.dt.uint16
U8 = mybir.dt.uint8
FP8X4 = mybir.dt.float8_e4m3fn_x4
ALU = mybir.AluOpType
ACT = mybir.ActivationFunctionType
AXIS_X = mybir.AxisListType.X

P = 128
PACK = 4
QUADRANT = 32
LINE = 4
PER_COLUMN = 16
GROUP = J // G
HALF = J // 2
QUARTER = J // 4
HALF_GROUPS = HALF // GROUP
QUARTER_GROUPS = QUARTER // GROUP
ALIGN = 64
LAST_SPLIT = QUARTER // 2


def interleave(copy, grouped, raw):
    copy(
        out=grouped.rearrange("p (line i) t -> p line t i", i=LINE),
        in_=raw.rearrange("p t (line i) -> p line t i", i=LINE),
    )


def quantize(nc, codes, scales, grouped):
    nc.vector.quantize_mx(
        out=codes.bitcast(FP8X4), scales=scales, in_=grouped.rearrange("p w t -> p (w t)")
    )


def one_pass(nc, result, weight_codes, weight_scales, codes, scales):
    nc.tensor.matmul_mx(
        result,
        lhsT=weight_codes.bitcast(FP8X4),
        lhsT_scale=weight_scales,
        rhs=codes.bitcast(FP8X4),
        rhs_scale=scales,
        start=True,
        stop=True,
    )


def by_group(ap):
    return ap.rearrange("p (g i) -> p g i", i=GROUP)


def spread(ap):
    return ap.unsqueeze(2).to_broadcast([P, ap.shape[1], GROUP])


def groups_of(ap, qt):
    return ap[:, qt * QUARTER_GROUPS : (qt + 1) * QUARTER_GROUPS]


def tile_attend_csqueeze_kernel(tc, tab_words, tab_scales, w1, steep, bias, wo, dy, old, offs, out):
    nc = tc.nc
    with ExitStack() as ctx:
        keep = ctx.enter_context(tc.tile_pool(name="keep", bufs=1))
        psum = ctx.enter_context(tc.psum_pool(name="psum", bufs=1))

        def new_tile(name, shape, dtype):
            return keep.tile(shape, dtype, name=name, align_bytes=ALIGN)[:]

        def new_tiles(stem, shape, dtype, count):
            return [new_tile("%s%d" % (stem, n), shape, dtype) for n in range(count)]

        offsets = keep.tile([P, J // PER_COLUMN], U16, name="offsets")
        tab_s = new_tile("tab_s", [P, T], U8)
        tab_w = new_tile("tab_w", [P, T], U32)
        w1_raw = new_tile("w1_raw", [P, PACK, R], F32)
        wo_raw = new_tile("wo_raw", [P, PACK, R], F32)
        dy_raw = new_tiles("dy_raw", [P, PACK, HALF], F32, 2)
        old_sb = new_tile("old_sb", [P, J], F32)
        rows = new_tile("rows", [P, QUADRANT], F32)

        nc.vector.memset(tab_s.bitcast(I32), 0)
        nc.vector.memset(rows, 0.0)
        nc.sync.dma_start(w1_raw, w1.rearrange("(p t) r -> p t r", t=PACK))
        nc.sync.dma_start(offsets[:], offs)
        scale_rows = tab_scales[0].bitcast(I32)
        for q in (0, 2, 1, 3):
            nc.sync.dma_start(
                tab_s[QUADRANT * q : QUADRANT * q + 4, :].bitcast(I32), scale_rows[4 * q : 4 * q + 4, :]
            )
        nc.sync.dma_start(tab_w.bitcast(I32), tab_words[0].rearrange("p n t -> p (n t)").bitcast(I32))
        nc.sync.dma_start(wo_raw, wo.rearrange("(p t) r -> p t r", t=PACK))
        nc.sync.dma_start(rows[0:P:QUADRANT, :], steep.rearrange("(q i) o -> q (i o)", i=QUADRANT))
        nc.sync.dma_start(rows[1:P:QUADRANT, :], bias.rearrange("(q i) o -> q (i o)", i=QUADRANT))
        warm = new_tile("warm", [P, 1], F32)
        warm_out = new_tile("warm_out", [P, 1], F32)
        nc.vector.memset(warm, 0.0)
        nc.scalar.activation(warm_out, warm, ACT.Sigmoid)
        dy_planes = dy.rearrange("(p t) j -> p t j", t=PACK)
        for h in range(2):
            nc.sync.dma_start(dy_raw[h], dy_planes[:, :, h * HALF : (h + 1) * HALF])
        nc.sync.dma_start(old_sb, old)

        got_s = new_tile("got_s", [P, J], U8)
        nc.vector.tensor_copy(got_s, tab_s.indirect(offsets[:]))

        w1_bf = new_tile("w1_bf", [P, R, PACK], BF16)
        w1_c, w1_s = new_tile("w1_c", [P, R], U32), new_tile("w1_s", [P, R], U8)
        interleave(nc.vector.tensor_copy, w1_bf, w1_raw)
        quantize(nc, w1_c, w1_s, w1_bf)

        a_ps = [psum.tile([P, HALF], F32, name="a_ps%d" % h)[:] for h in range(2)]
        got_w = new_tiles("got_w", [P, HALF], U32, 2)
        half_columns = HALF // PER_COLUMN
        for h in range(2):
            half_offsets = offsets[:, h * half_columns : (h + 1) * half_columns]
            nc.vector.tensor_copy(got_w[h], tab_w.indirect(half_offsets))
            one_pass(nc, a_ps[h], w1_c, w1_s, got_w[h], got_s[:, h * HALF : (h + 1) * HALF])

        wo_bf = new_tile("wo_bf", [P, R, PACK], BF16)
        wo_c, wo_s = new_tile("wo_c", [P, R], U32), new_tile("wo_s", [P, R], U8)
        interleave(nc.scalar.copy, wo_bf, wo_raw)
        quantize(nc, wo_c, wo_s, wo_bf)

        columns = new_tile("columns", [P, QUADRANT], F32)
        slope = new_tile("slope", [P, 1], F32)
        nc.vector.transpose(columns, rows)
        nc.gpsimd.tensor_scalar(slope, columns[:, 0:1], 1.0 / GROUP, 0.0, ALU.mult, ALU.add)

        dy_bf = new_tiles("dy_bf", [P, QUARTER, PACK], BF16, 4)
        dy_c, dy_s = new_tiles("dy_c", [P, QUARTER], U32, 4), new_tiles("dy_s", [P, QUARTER], U8, 4)
        c0_ps = [psum.tile([P, QUARTER], F32, name="c0_ps%d" % qt)[:] for qt in range(4)]
        sums, neg_deriv = new_tile("sums", [P, G], F32), new_tile("neg_deriv", [P, G], F32)
        neg_a_w = new_tiles("neg_a_w", [P, QUARTER], F32, 4)
        with_old, res = new_tiles("with_old", [P, QUARTER], F32, 4), new_tiles("res", [P, QUARTER], F32, 4)

        def freed(qt, t, width):
            first = (qt % 2) * QUARTER
            return dy_raw[qt // 2][:, t, first : first + width]

        gate = freed(1, 0, G)
        prod = [freed(2, 0, QUARTER) if qt == 1 else new_tile("prod%d" % qt, [P, QUARTER], F32) for qt in range(4)]
        gated = [freed(2, 1, QUARTER) if qt == 1 else new_tile("gated%d" % qt, [P, QUARTER], F32) for qt in range(4)]
        e1 = [freed(2, 2, QUARTER_GROUPS)] + new_tiles("e1_", [P, QUARTER_GROUPS], F32, 3)

        def weigh(qt):
            first = (qt % 2) * QUARTER
            nc.vector.scalar_tensor_tensor(
                by_group(neg_a_w[qt]),
                by_group(a_ps[qt // 2][:, first : first + QUARTER]),
                slope,
                spread(groups_of(neg_deriv, qt)),
                ALU.mult,
                ALU.mult,
            )

        def round_dy(qt, lo, hi, copy):
            first = (qt % 2) * QUARTER
            interleave(copy, dy_bf[qt][:, lo:hi, :], dy_raw[qt // 2][:, :, first + lo : first + hi])

        def second_product(qt):
            quantize(nc, dy_c[qt], dy_s[qt], dy_bf[qt])
            one_pass(nc, c0_ps[qt], wo_c, wo_s, dy_c[qt], dy_s[qt])

        def multiply(qt):
            nc.vector.tensor_tensor(prod[qt], c0_ps[qt], neg_a_w[qt], ALU.mult)
            nc.vector.tensor_tensor(by_group(gated[qt]), by_group(c0_ps[qt]), spread(groups_of(gate, qt)), ALU.mult)

        def group_dots(qt):
            nc.vector.tensor_reduce(e1[qt], by_group(prod[qt]), AXIS_X, ALU.add, negate=True)

        def add_old(qt, engine):
            engine.tensor_tensor(with_old[qt], gated[qt], old_sb[:, qt * QUARTER : (qt + 1) * QUARTER], ALU.add)

        def store(qt):
            nc.sync.dma_start(out[:, qt * QUARTER : (qt + 1) * QUARTER], res[qt])

        def finish_on_scalar(qt):
            for g in range(QUARTER_GROUPS):
                cols = slice(g * GROUP, (g + 1) * GROUP)
                nc.scalar.activation(res[qt][:, cols], with_old[qt][:, cols], ACT.Identity, bias=e1[qt][:, g : g + 1])
            store(qt)

        def finish_on_vector(qt):
            nc.vector.tensor_tensor(by_group(res[qt]), by_group(with_old[qt]), spread(e1[qt]), ALU.add)
            store(qt)

        for h in range(2):
            half_sums = sums[:, h * HALF_GROUPS : (h + 1) * HALF_GROUPS]
            nc.vector.tensor_reduce(half_sums, by_group(a_ps[h]), AXIS_X, ALU.add)
        round_dy(0, 0, QUARTER, nc.vector.tensor_copy)
        round_dy(1, 0, QUARTER, nc.scalar.copy)
        nc.scalar.activation(gate, sums, ACT.Sigmoid, bias=columns[:, 1:2], scale=slope)
        second_product(0)
        second_product(1)
        nc.vector.scalar_tensor_tensor(neg_deriv, gate, 1.0, gate, ALU.subtract, ALU.mult)
        weigh(0)
        weigh(1)

        round_dy(2, 0, QUARTER, nc.scalar.copy)
        round_dy(3, 0, LAST_SPLIT, nc.scalar.copy)
        multiply(0)
        add_old(0, nc.gpsimd)
        round_dy(3, LAST_SPLIT, QUARTER, nc.vector.tensor_copy)
        weigh(2)
        weigh(3)
        second_product(2)
        second_product(3)
        multiply(1)
        add_old(1, nc.gpsimd)
        for qt in range(2):
            group_dots(qt)
            finish_on_scalar(qt)

        multiply(2)
        add_old(2, nc.gpsimd)
        multiply(3)
        group_dots(2)
        group_dots(3)
        add_old(3, nc.vector)
        finish_on_vector(2)
        finish_on_vector(3)
